import numpy as np, ml_dtypes
CORES = [9,25,41,57]
N = 4
BF = ml_dtypes.bfloat16
def gentries(a):
    return np.ascontiguousarray(a.reshape(8, 16, -1).transpose(0, 2, 1)).reshape(8, -1)
def gtable(e):
    e = np.asarray(e); return np.ascontiguousarray(e.reshape(8, -1, 16).transpose(0, 2, 1)).reshape(128, -1).astype(np.int32)
W, Q, RO, END = 2048, 1024, 4, 2 ** 20 - 1
def rise(rng, n, lo, hi, e):
    return lo + (np.sort(rng.random(n)) ** e * (hi - lo - n)).astype(np.int64) + np.arange(n)
def split(rng, w, total):
    return 1 + rng.multinomial(total - len(w), np.minimum(w * np.reciprocal(np.sum(w)), 1.0))
def families(rng, L, dev, e, total):
    u = np.exp2(dev * rng.standard_normal(L)); nb0 = split(rng, u, total); like = rng.random(L) < 0.6; like[0] = True; like[1] = False
    rest = total - int(np.sum(nb0[like])); m = L - int(np.sum(like)); nb = np.tile(nb0, (N, 1))
    for r in range(N): nb[r, ~like] = split(rng, u[~like] * np.exp2(2 * rng.standard_normal(m)), rest)
    pad = rng.integers(1, 17, (N, L)); top = np.max(16 * nb - pad, axis=0); base = []
    for l in range(L):
        t = int(top[l]); more = (0, 1, t // 16)[int(rng.integers(0, 3))] if like[l] else t // 8
        base.append(rise(rng, max(1, t + more), 0, END, e))
    return nb, pad, base
def lay(rng, nb, pad, base, mode):
    ids = np.full((N, W * 16), END, np.int64); fst = np.zeros(nb.shape, np.int64)
    for r in range(N):
        at = 0
        for l in rng.permutation(nb.shape[1]):
            b = base[l]; n = int(nb[r, l]); c = 16 * n - int(pad[r, l]); fst[r, l] = at
            if c > 0:
                if mode == 1: v = b[len(b) - c:]
                else:
                    ix = np.sort(rng.permutation(len(b))[:c])
                    if mode == 2:
                        ix[-1] = len(b) - 1
                        if c > 1: ix[0] = 0
                    v = b[ix]
                ids[r, 16 * at:16 * at + c] = v
            at += n
    return np.ascontiguousarray(ids.reshape(N, W, 16).transpose(0, 2, 1)), fst
def starts(rng, nb, fst):
    L = nb.shape[1]; f = np.tile(rng.integers(0, L, Q), (N, 1))
    f = np.where((rng.random((N, Q)) < 0.5) & (rng.random(Q) < 0.125), rng.integers(0, L, (N, Q)), f)
    u = np.where(rng.random(Q) < 0.125, rng.random((N, Q)), rng.random(Q) * (rng.random(Q) < 0.5))
    m = np.take_along_axis(nb, f, 1)
    return np.take_along_axis(fst, f, 1) + np.minimum((u * m).astype(np.int64), m - 1)
def follow(a):
    last = np.concatenate([a[..., 15, :], np.full(a.shape[:-2] + (16,), END, a.dtype)], axis=-1)
    t = np.empty(a.shape, a.dtype); t[..., 0, :] = last[..., :W]
    for i in range(1, 16): t[..., i, :] = np.where(t[..., i - 1, :] == END, END, last[..., i:i + W])
    return t
def pack(ids, st):
    a = np.stack(ids, axis=1); s = np.stack(st, axis=1)
    return {"ids": a.reshape(N, 128, W).astype(np.int32), "tops": follow(a).reshape(N, 128, W).astype(np.int32), "st": np.stack([gtable(x) for x in s])}
def setup_inputs(rng):
    ids, st = [], []
    for g in range(8):
        nb, pad, base = families(rng, int(rng.integers(12, 49)), 1.5, 1.0, W)
        a, fst = lay(rng, nb, pad, base, 0); ids.append(a); st.append(starts(rng, nb, fst))
    return pack(ids, st)
def setup_inputs_far(rng):
    ids, st = [], []; dl = np.array([0, 1, 15, 16, 17, 31, 32, 33])
    for g in range(8):
        L = 6; nb = np.tile(63 + split(rng, rng.random(L) + 0.5, W - 63 * L), (N, 1)); pad = np.tile(rng.integers(1, 17, L), (N, 1))
        base = [rise(rng, int(16 * nb[0, l] - pad[0, l]), 0, END, 1.0) for l in range(L)]
        a, fst = lay(rng, nb, pad, base, 0)
        f = rng.integers(0, L, Q); k = 33 + (rng.random(Q) * (nb[0][f] - 34)).astype(np.int64)
        d = dl[rng.integers(0, np.where(rng.random(Q) < 0.75, 4, 8), (N, Q))]; d[:, :8] = dl
        d[rng.integers(0, N, Q), np.arange(Q)] = 0
        ids.append(a); st.append(np.take_along_axis(fst, np.tile(f, (N, 1)), 1) + k - d)
    return pack(ids, st)
def setup_inputs_ends(rng):
    ids, st = [], []
    for g in range(8):
        nb, pad, base = families(rng, W // 16, 2.0, 1.0, W - 5)
        base = [rise(rng, 1, 0, END, 1.0), np.array([END - 1]), np.array([0, END - 1]), np.array([0, int(rng.integers(1, END - 1)), END - 1]), rise(rng, 15, 0, END, 1.0)] + base
        for b in base[4:]:
            b[0] = 0; b[-1] = END - 1
        nb = np.concatenate([np.ones((N, 5), np.int64), nb], axis=1); pad = np.concatenate([np.tile(np.array([16, 15, 14, 13, 1]), (N, 1)), pad], axis=1)
        a, fst = lay(rng, nb, pad, base, 2); L = nb.shape[1]
        f = np.tile(np.where(rng.random(Q) < 0.25, rng.integers(0, 5, Q), rng.integers(0, L, Q)), (N, 1))
        k = np.where(rng.random(Q) < 0.75, rng.integers(0, 3, Q), rng.integers(0, 3, (N, Q)))
        m = np.take_along_axis(nb, f, 1); s = np.take_along_axis(fst, f, 1) + np.where(k == 0, 0, np.maximum(m - k, 0))
        s[:, 0] = 0; s[:, 1] = W - 1
        ids.append(a); st.append(s)
    return pack(ids, st)
def setup_inputs_alike(rng):
    ids, st = [], []
    for g in range(8):
        L = int(rng.integers(8, 21)); nb = np.tile(split(rng, rng.random(L) + 0.2, W), (N, 1)); pad = rng.integers(1, 17, (N, L)); base = []
        for l in range(L):
            b = np.add.accumulate(rng.choice(np.array([1, 1, 1, 1, 2, 5]), int(16 * nb[0, l] - 1)))
            base.append(b - b[-1] + END - 1 if l % 2 == 0 else b - b[0] + int(rng.integers(0, END - int(b[-1] - b[0]))))
        a, fst = lay(rng, nb, pad, base, 1)
        f = rng.integers(0, L, Q); k = (rng.random(Q) * nb[0][f]).astype(np.int64)
        if g % 2 == 1:
            i = rng.integers(0, 3, Q); f = f[i]; k = k[i]
        ids.append(a); st.append(np.take_along_axis(fst, np.tile(f, (N, 1)), 1) + k)
    return pack(ids, st)
def marks(rng, n):
    k = np.sort(rng.permutation(n // 16 - 1)[:15]) + 1; i = np.concatenate([np.array([-1]), 16 * k, np.array([n])]); v = []
    for m in range(16):
        p = rise(rng, int(i[m + 1] - i[m] - 1), 65536 * m, 65536 * m + 65535, 1.0)
        if rng.random() < 0.5: p[0] = 65536 * m
        v += [p, np.array([65536 * m + 65535])]
    return np.concatenate(v)[:-1]
def runs(n):
    h = n // 16 + 1
    return np.concatenate([np.arange(65536 * m - h // 2, 65536 * m - h // 2 + h) for m in range(1, 16)] + [np.arange(END - h, END)])
def setup_inputs_cases(rng):
    ids, st = [], []; L = 6; al = np.arange(L); aq = np.arange(Q); kinds = rng.permutation(8)
    for g in range(8):
        z = int(kinds[g]); nb = np.tile(63 + split(rng, rng.random(L) + 0.5, W - 63 * L), (N, 1)); m = nb[0]
        pad = np.tile(rng.integers(1, 17, L), (N, 1)); q = rng.integers(0, N, L); add = np.zeros((N, L), np.int64)
        if z == 0:
            add = 65536 * np.stack([rng.permutation(8)[:N] for l in range(L)], axis=1); add[:, 0] = 0; add[q[0], 0] = 65536
        if z == 2:
            add[:] = 1; add[q, al] = 0
        if z == 3:
            pad[:, :3] = 1; pad[q[:3], al[:3]] = 16; pad[:, 3:] = 16; add[q[3:], al[3:]] = 2 ** 19
        base = []
        for l in range(L):
            c = int(16 * m[l] - np.min(pad[:, l]))
            if z == 0: base.append(rise(rng, c, 0, 2 ** 19, 1.0))
            elif z == 1: base.append(marks(rng, c))
            elif z == 2: base.append(rise(rng, c, 1000100, END - 1, 1.0))
            elif z == 3 and l >= 3: base.append(rise(rng, c, 0, 2 ** 18, 1.0))
            elif z == 7: base.append(runs(c * 9 // 8))
            else: base.append(rise(rng, c, 0, END, 1.0))
        a, fst = lay(rng, nb, pad, base, 0 if z == 7 else 1)
        for r in range(N):
            for l in range(L):
                s = int(fst[r, l]); x = a[r, :, s:s + int(m[l])]
                a[r, :, s:s + int(m[l])] = np.where(x < END, x + add[r, l], END)
        f = rng.integers(0, L, Q); u = rng.random(Q); k = (u * m[f]).astype(np.int64); d = np.zeros((N, Q), np.int64)
        if z == 1:
            mk = np.stack([np.flatnonzero(b % 65536 == 65535) // 16 for b in base]); k = np.where(rng.random(Q) < 0.75, mk[f, rng.integers(0, 15, Q)], k)
        if z == 3:
            e = f >= 3; k = np.where(e, m[f] - 1, 16 + (u * (m[f] - 17)).astype(np.int64))
            d = np.where(rng.random((N, Q)) < 0.5, 15, rng.integers(0, 17, (N, Q))); d[:, :Q // 4] = 15; d = np.where(e, 16, d)
            d[q[f], aq] = np.where(e, k - rng.integers(0, 8, Q), 0)
        if z == 4:
            k = 16 + (u * (m[f] - 18)).astype(np.int64); d[q[0]] = rng.integers(1, 17, Q)
        if z == 5:
            o = rng.permutation(W)[:Q]; f = np.repeat(al, m)[o]; k = (np.arange(W) - np.repeat(np.add.accumulate(m) - m, m))[o]
        if z == 6:
            f[:] = int(np.argmax(fst[0])); k = 16 + (u[0] * (m[f] - 18)).astype(np.int64); d = np.tile(rng.integers(0, 17, (N, 1)), (1, Q)); d[q[0]] = 0
        if z == 7:
            k = np.maximum(k, 1); d = rng.integers(0, 2, (N, Q))
        ids.append(a); st.append(np.take_along_axis(fst, np.tile(f, (N, 1)), 1) + k - d)
    return pack(ids, st)
def setup_inputs_spread(rng):
    ids, st = [], []
    for g in range(8):
        nb, pad, base = families(rng, int(rng.integers(4, 65)), 3.0, float(rng.choice(np.array([1.0, 3.0, 8.0]))), W)
        a, fst = lay(rng, nb, pad, base, 0); s = starts(rng, nb, fst)
        ids.append(a); st.append(np.where(rng.random(Q) < 0.25, rng.integers(0, W, (N, Q)), s))
    return pack(ids, st)
def check_inputs(d):
    bad = []
    for k, lo, hi in (("ids", 0, END), ("st", 0, W - 1)):
        if np.min(d[k]) < lo or np.max(d[k]) > hi: bad.append("range of " + k)
    a = d["ids"].astype(np.int64).reshape(N, 8, 16, W); x, y = a[:, :, :-1], a[:, :, 1:]
    if not np.all((y > x) | ((x == END) & (y == END))): bad.append("order inside a block of ids")
    x, y = a[:, :, 15, :-1], a[:, :, 0, 1:]
    if not np.all((y > x) | (x == END)): bad.append("order from block to block of ids")
    if not np.all(a[:, :, 15, W - 1] == END): bad.append("end of the last list of ids")
    if not np.array_equal(d["tops"].astype(np.int64).reshape(N, 8, 16, W), follow(a)): bad.append("tops")
    return bad
def reference(ids, tops, st):
    a = ids.astype(np.int64).reshape(N, 8, 16, W); t = tops.astype(np.int64).reshape(N, 8, 16, W)
    b = np.stack([gentries(x) for x in st]).astype(np.int64)
    cur = np.take_along_axis(a[:, :, 0], b, 2)
    hits = np.zeros((8, Q), np.int64); total = np.zeros((8, Q), np.int64)
    for rnd in range(RO):
        v = np.max(cur, axis=0); hit = (np.min(cur, axis=0) == v) & (v < END)
        hits = hits + hit; total = total + np.where(hit, v, 0); v = v + hit
        n = np.sum(np.take_along_axis(t, b[:, :, None, :], 3) < v[None, :, None, :], axis=2)
        b = b + n
        x = np.take_along_axis(a, b[:, :, None, :], 3)
        p = np.sum(x < v[None, :, None, :], axis=2)
        cur = np.take_along_axis(x, np.minimum(p, 15)[:, :, None, :], 2)[:, :, 0]
    return {"yh": np.stack([gtable(hits)] * N).astype(np.float32), "ys": np.stack([gtable(total)] * N).astype(np.float32),
            "yb": np.stack([gtable(x) for x in b]).astype(np.float32), "yc": np.stack([gtable(x) for x in cur]).astype(np.float32)}

@@ -1,0 +1,349 @@
+from concourse.bass import DstId, RemoteDMATransfer
+from concourse.mybir import AluOpType, ActivationFunctionType
+
+NR = 4
+RO = 4
+W = 2048
+END = 2 ** 20 - 1
+BIG = float(2 ** 21)
+FILL_V = 1024
+FILL_S = 640
+TOP0 = 512
+NCS = 70
+NDS = 34
+
+SCRATCH = {n: ("sbuf", [128, c], d) for n, c, d in [
+    ("sti", 64, "int32"), ("off", 64 * (RO + 1), "uint16"), ("bF", 64 * (RO + 1), "float32"),
+    ("W0", W, "int32"), ("TI", W, "int32"), ("XI", W, "int32"),
+    ("Tg", 1024, "float32"), ("Xg", 1024, "float32"), ("Yw", 1024, "float32"),
+    ("C1", 1024, "bfloat16"), ("C2", 1024, "bfloat16"),
+    ("land", RO * 2 * NR * 32, "float32"), ("nar", 2 * 8 * 32, "float32"), ("HS", 128, "float32"), ("curT", 64, "float32"),
+    ("HL", 196, "float16"), ("PT", 256, "float16"), ("OH", 256, "float32"), ("OC", 256, "float32"),
+    ("kI", 4, "int32"), ("kF", 16, "float32"), ("tF", 144, "float32"), ("td", 512, "float32"), ("tp", 128, "float32"),
+    ("Bc", 144, "bfloat16"), ("sA", 128, "float32"), ("sB", 128, "float32"), ("Sel", 128, "bfloat16"),
+    ("Wall", 512, "float16"), ("I16", 128, "float16"), ("I32", 128, "float32"), ("P32", 128, "float32"), ("Rm", 8, "float32")]}
+SCRATCH.update({n: ("psum", [128, 512], "float32") for n in ["PW00", "PW01", "PW10", "PW11", "NA0", "NA1", "NB0", "NB1"]})
+SEMAPHORES = (["c%d" % i for i in range(NCS)] + ["d%d" % i for i in range(NDS)] + ["sent"]
+              + ["a%d_%d_%d" % (r, ch, s) for r in range(RO) for ch in range(2) for s in range(NR)])
+
+
+def emit(ops, Q, T):
+    writers, readers, bank = {}, {}, {}
+    known = {q: 0 for q in Q}
+    for n, op in enumerate(ops):
+        q = op["q"]
+        deps = set()
+        for k in op["r"]:
+            deps.update(writers.get(k, []))
+        for k in op["w"]:
+            deps.update(readers.get(k, []))
+            deps.update(writers.get(k, []))
+        for b in op["b"]:
+            run = bank.get(b)
+            if run is None or run[0] != q:
+                if run is not None:
+                    deps.update(run[1])
+                bank[b] = (q, [n], run[1] if run is not None else [])
+            else:
+                deps.update(run[2])
+                run[1].append(n)
+        if q == "p":
+            deps = set(d for d in deps if ops[d]["q"] != "p")
+        deps.discard(n)
+        waits = []
+        for d in sorted(deps, reverse=True):
+            if not (known[q] >> d) & 1:
+                waits.append(d)
+                ops[d]["waited"] = True
+                known[q] |= ops[d]["hb"] | (1 << d)
+        op["waits"] = waits
+        op["hb"] = known[q]
+        for k in op["r"]:
+            readers.setdefault(k, []).append(n)
+        for k in op["w"]:
+            if op["acc"]:
+                writers.setdefault(k, []).append(n)
+            else:
+                writers[k] = [n]
+            readers[k] = []
+    pools = {False: [["c%d" % i, -1, 0] for i in range(NCS)], True: [["d%d" % i, -1, 0] for i in range(NDS)]}
+    for n, op in enumerate(ops):
+        eng = Q[op["q"]]
+        for d in reversed(op["waits"]):
+            eng.wait_ge(T.sem[ops[d]["sem"]], ops[d]["val"])
+        for name, val in op["ext"]:
+            eng.wait_ge(T.sem[name], val)
+        slot = None
+        if op["waited"]:
+            for s in pools[op["dma"]]:
+                if s[1] < 0 or (op["hb"] >> s[1]) & 1:
+                    slot = s
+                    break
+            assert slot is not None
+        for f in op["fn"]:
+            ins = f()
+            if slot is not None:
+                inc = 16 if op["dma"] else 1
+                ins.then_inc(T.sem[slot[0]], inc)
+                slot[2] += inc
+        if slot is not None:
+            slot[1] = n
+            op["sem"], op["val"] = slot[0], slot[2]
+
+
+def rank_program(g, core, T, topo):
+    rank = T.rank_of(core)
+    if rank is None:
+        return
+    A = AluOpType
+    ACT = ActivationFunctionType
+    V, S, P, Y = g.vector, g.scalar, g.tensor, g.sync
+    Q = {"v": V, "s": S, "p": P, "g": g, "y": Y}
+    ops = []
+
+    def add(q, fn, r=(), w=(), b=(), ext=(), dma=False, acc=False):
+        ops.append({"q": q, "fn": fn if isinstance(fn, list) else [fn], "r": list(r), "w": list(w), "b": list(b),
+                    "ext": list(ext), "dma": dma, "acc": acc, "waited": False})
+
+    def ts(out, in0, s1, s2, o0, o1, r, w, b=()):
+        if o1 is None:
+            add("v", lambda: V.tensor_scalar(out, in0, s1, None, o0), r, w, b)
+        else:
+            add("v", lambda: V.tensor_scalar(out, in0, s1, s2, o0, o1), r, w, b)
+
+    def tt(out, in0, in1, o, r, w, b=(), ext=()):
+        add("v", lambda: V.tensor_tensor(out, in0, in1, o), r, w, b, ext)
+
+    def cp(out, in_, r, w, b=()):
+        add("v", lambda: V.tensor_copy(out, in_), r, w, b)
+
+    def act(out, in_, r, w, b=(), scale=1.0, bias=None):
+        if bias is None:
+            add("s", lambda: S.activation(out, in_, ACT.Identity, scale=scale), r, w, b)
+        else:
+            add("s", lambda: S.activation(out, in_, ACT.Identity, bias=bias), r, w, b)
+
+    def mm(out, lhsT, rhs, start=True, stop=True):
+        return lambda: P.matmul(out, lhsT, rhs, start, stop)
+
+    def dma(q, out, in_, r, w, ext=()):
+        add(q, lambda: Q[q].dma_start(out, in_), r, w, (), ext, dma=True)
+
+    def iota(out, pattern, key):
+        add("g", lambda: g.iota(out, pattern, 0, 0, allow_small_or_imprecise_dtypes=True), w=[key])
+
+    peers = [(rank + k) % NR for k in range(1, NR)]
+    srcs = [(rank - k) % NR for k in range(1, NR)]
+    mask = topo.mask(core, T.cores[peers[0]])
+    for p in peers:
+        mask &= topo.mask(core, T.cores[p])
+    neng = bin(mask).count("1")
+    dst_ids = []
+    for p in peers:
+        a = topo.addr(T.cores[p])
+        dst_ids.append(DstId(rid=a[0], pnc=a[1]))
+
+    def slot(r, ch, s):
+        c = ((r * 2 + ch) * NR + s) * 32
+        return T.land[:, c:c + 32]
+
+    def send(r, ch):
+        sl = slot(r, ch, rank)
+        tr = RemoteDMATransfer(dst_ids=dst_ids, dma_engine_mask=mask, remote_sem=T.sem["a%d_%d_%d" % (r, ch, rank)],
+                               srcs=[sl], dsts=[sl] * len(dst_ids))
+        add("g", lambda: g.remote_dma_fused([tr], local_sem=T.sem.sent), r=[("own", r, ch)])
+
+    PW = [[T.PW00, T.PW01], [T.PW10, T.PW11]]
+    NA = [T.NA0, T.NA1]
+    NB = [T.NB0, T.NB1]
+    kF = T.kF
+    K, KA, KM, K32, BG, NX, KK, K32B, TMP, WC = [kF[:, i:i + 1] for i in range(10)]
+
+    def offs(r, ch, h=None):
+        c = r * 64 + ch * 32
+        return T.off[:, c:c + 32] if h is None else T.off[:, c + 16 * h:c + 16 * h + 16]
+
+    def wide(buf, ch, h=None):
+        c = ch * 512
+        return buf[:, c:c + 512] if h is None else buf[:, c + 256 * h:c + 256 * h + 256]
+
+    def par(buf, ch, s):
+        return buf[:, ch * 512 + s:ch * 512 + 512:2]
+
+    def quarter(buf, ch, s):
+        return buf[:, ch * 512 + s:ch * 512 + 512:4]
+
+    def redcol(ch, s):
+        return NB[ch][:, 8 * s:8 * s + 8]
+
+    def narc(ch, i):
+        c = (ch * 8 + i) * 32
+        return T.nar[:, c:c + 32]
+
+    def gather_tops(r, ch):
+        act(wide(T.Tg, ch), T.TI[:, 0:W].indirect(offs(r, ch)), ["T0", "T1", ("off", r, ch), "BG"], [("Tg", ch)], bias=BG)
+
+    def clip(r, ch):
+        ts(narc(ch, 6), slot(r, ch, rank), (END - 1) / 32.0, None, A.min, None, [("own", r, ch)], [("nar", ch, 6)])
+
+    dma("y", T.sti[:, :], T.st[:, :], [], ["sti"])
+    dma("y", T.TI[:, 0:TOP0], T.tops[:, 0:TOP0], [], ["T0"])
+    add("v", lambda: V.memset(T.W0[:, 0:256], 0), w=["W0a"])
+    add("v", lambda: V.memset(T.W0[:, 256:FILL_V], 0), w=["W0b"])
+    add("g", lambda: g.iota(T.W0[:, FILL_V + FILL_S:W], [[0, W - FILL_V - FILL_S]], 0, 0), w=["W0c"])
+    w0 = ["W0a", "W0b", "W0c"]
+    for c in range(FILL_V, FILL_V + FILL_S, 256):
+        n = min(256, FILL_V + FILL_S - c)
+        act(T.W0[:, c:c + n], T.W0[:, 0:n], ["W0a"], [("W0", c)])
+        w0.append(("W0", c))
+    dma("y", T.W0[0:128:16, :], T.ids[0:128:16, :], [], w0)
+    dma("y", T.TI[:, TOP0:W], T.tops[:, TOP0:W], [], ["T1"])
+    dma("y", T.XI[:, :], T.ids[:, :], [], ["X"])
+    add("g", lambda: g.iota(T.kI[:, 0:1], [[0, 1]], 0, 1), w=["k0"])
+    iota(T.tF[:, :], [[1, 144]], "tF")
+    iota(T.td[:, :], [[1, 32], [0, 16]], "td")
+    ts(T.kI[:, 1:2], T.kI[:, 0:1], 112, None, A.bitwise_and, None, ["k0"], ["k1"])
+    ts(T.kI[:, 2:3], T.kI[:, 0:1], 15, None, A.bitwise_and, None, ["k0"], ["k2"])
+    ts(T.kI[:, 3:4], T.kI[:, 0:1], 31, None, A.bitwise_and, None, ["k0"], ["k3"])
+    cp(kF[:, 0:4], T.kI[:, 0:4], ["k0", "k1", "k2", "k3"], ["kF"])
+    ts(BG, KM, 15.0, BIG, A.is_equal, A.mult, ["kF"], ["BG"])
+    ts(K32B, K, 96.0, 1000.0, A.is_ge, A.mult, ["kF"], ["K32B"])
+    ts(WC, K, 64.0, 31.0, A.is_lt, A.mult, ["kF"], ["WC"])
+    ts(T.Rm[:, :], T.tF[:, 0:128:16], KA, 1.0 / 32, A.is_equal, A.mult, ["tF", "kF"], ["Rm"])
+    cp(T.off[:, 0:64], T.sti[:, :], ["sti"], [("off", 0, 0), ("off", 0, 1)])
+    cp(T.bF[:, 0:64], T.sti[:, :], ["sti"], [("bF", 0, 0), ("bF", 0, 1)])
+    ts(TMP, BG, -16.0 / BIG, 1.0, A.mult, A.add, ["BG"], ["TMP"])
+    tt(KK, BG, K, A.add, ["BG", "kF"], ["KK"])
+    tt(K32B, K32B, K32, A.add, ["K32B", "kF"], ["K32B"])
+    tt(NX, TMP, K, A.add, ["TMP", "kF"], ["NX"])
+    ts(WC, WC, 1.0, None, A.add, None, ["WC"], ["WC"])
+    for ch in range(2):
+        for h in range(2):
+            win = T.W0[:, 0:W].indirect(offs(0, ch, h))
+            (act if h else cp)(wide(T.Xg, ch, h), win, w0 + [("off", 0, ch)], [("Xg", ch, h)])
+    for ch in range(2):
+        add("p", [mm(redcol(ch, s), quarter(T.Xg, ch, s), T.Rm[:, :]) for s in range(4)],
+            r=[("Xg", ch, 0), ("Xg", ch, 1), "Rm"], w=[("red", ch, s) for s in range(4)], b=[("NB", ch)])
+        cp(slot(0, ch, rank), NB[ch][:, 0:32], [("red", ch, s) for s in range(4)], [("own", 0, ch)], [("NB", ch)])
+        send(0, ch)
+        if ch == 0:
+            ts(T.HL[:, 96:196:98], kF[:, 0:2], 0.0, 32768.0, A.mult, A.add, ["kF"], ["HLc"])
+            ts(T.Bc[:, :], T.tF[:, :], 15.0, KA, A.subtract, A.is_equal, ["tF", "kF"], ["Bc"])
+            ts(T.I16[:, :], T.tF[:, 0:128], K, None, A.is_equal, None, ["tF", "kF"], ["I16"])
+    iota(T.tp[:, :], [[1, 4], [4, 32]], "tp")
+    ts(T.Wall[:, :], T.td[:, :], K32B, WC, A.is_equal, A.mult, ["td", "K32B", "WC"], ["Wall"])
+    ts(T.I32[:, :], T.tF[:, 0:128], K, None, A.is_equal, None, ["tF", "kF"], ["I32"])
+    ts(T.Wall[96:97, 15:512:16], T.td[96:97, 0:32], 0.0, 64.0, A.mult, A.add, ["td"], ["Wall"])
+    ts(T.sA[:, :], T.tF[:, 0:128], NX, None, A.is_equal, None, ["tF", "NX"], ["sA"])
+    ts(T.sB[:, :], T.tF[:, 0:128], KK, None, A.is_equal, None, ["tF", "KK"], ["sB"])
+    ts(T.P32[:, :], T.tp[:, :], K, None, A.is_equal, None, ["tp", "kF"], ["P32"])
+    tt(T.Sel[:, :], T.sA[:, :], T.sB[:, :], A.subtract, ["sA", "sB"], ["Sel"])
+    gather_tops(0, 0)
+    gather_tops(0, 1)
+    clip(0, 0)
+
+    for r in range(RO):
+        last = r == RO - 1
+        for ch in range(2):
+            def nar(i):
+                return narc(ch, i)
+
+            def nk(i):
+                return ("nar", ch, i)
+            hl = ch * 98
+            hi, lo, hit = [T.HL[:, hl + 32 * j:hl + 32 * j + 32] for j in range(3)]
+            mx, mn, mxk, mnk = slot(r, ch, rank), nar(6), ("own", r, ch), nk(6)
+            for j, s in enumerate(srcs):
+                arr = [("a%d_%d_%d" % (r, ch, s), neng)]
+                if j == NR - 2:
+                    tt(hi, mx, slot(r, ch, s), A.max, [mxk], [("hi", ch)], ext=arr)
+                    arr = []
+                tt(nar(j), mx, slot(r, ch, s), A.max, [mxk], [nk(j)], ext=arr)
+                tt(nar(3 + j), mn, slot(r, ch, s), A.min, [mnk], [nk(3 + j)])
+                mx, mn, mxk, mnk = nar(j), nar(3 + j), nk(j), nk(3 + j)
+            tt(lo, mx, hi, A.subtract, [mxk, ("hi", ch)], [("lo", ch)])
+            tt(hit, mx, mn, A.is_equal, [mxk, mnk], [("hit", ch)])
+            add("p", mm(NA[ch][0:97, 0:128], T.HL[:, hl:hl + 97], T.I16[:, :]),
+                r=[("hi", ch), ("lo", ch), ("hit", ch), "HLc", "I16"], w=[("tr", ch)], b=[("NA", ch)])
+            hcol = T.HS[:, ch * 64:ch * 64 + 32]
+            scol = T.HS[:, ch * 64 + 32:ch * 64 + 64]
+            if r == 0:
+                tt(scol, hit, mx, A.mult, [("hit", ch), mxk], [("Sm", ch)])
+            else:
+                tt(nar(7), hit, mx, A.mult, [("hit", ch), mxk], [nk(7)])
+            pt = T.PT[0:97, ch * 128:ch * 128 + 128]
+            cp(pt, NA[ch][0:97, 0:128], [("tr", ch)], [("PT", ch)], [("NA", ch)])
+            for s in range(2):
+                add("p", [mm(PW[ch][s][:, h:256:2], T.Wall[0:97, 128 * (2 * h + s):128 * (2 * h + s) + 128], pt)
+                          for h in range(2)], r=[("PT", ch), "Wall"], w=[("pw", ch, s)], b=[("PW", ch, s)])
+            cnt = NA[ch][:, 128:160]
+            bold = T.bF[:, r * 64 + ch * 32:r * 64 + ch * 32 + 32]
+            add("p", mm(cnt, T.I32[:, :], bold, True, False), r=["I32", ("bF", r, ch)], w=[("cnt", ch)], b=[("NA", ch)])
+            if r == 0:
+                cp(hcol, hit, [("hit", ch)], [("H", ch)])
+            else:
+                tt(hcol, hcol, hit, A.add, [("hit", ch), ("H", ch)], [("H", ch)])
+            for s in range(2):
+                c = ch * 512 + 256 * s
+                for h in range(2):
+                    tt(T.C1[:, c + h:c + 256:2], quarter(T.Tg, ch, 2 * h + s), PW[ch][s][:, h:256:2], A.is_lt,
+                       [("Tg", ch), ("pw", ch, s)], [("C1", ch, s, h)], [("PW", ch, s)])
+                    add("p", [mm(cnt, T.Bc[:, 15 - 2 * j - s:143 - 2 * j - s], T.C1[:, c + j:c + 256:8], False, s == 1 and j == 7)
+                              for j in range(h, 8, 2)], r=["Bc", ("C1", ch, s, h)], w=[("cnt", ch)], b=[("NA", ch)], acc=True)
+            if r > 0:
+                tt(scol, scol, nar(7), A.add, [nk(7), ("Sm", ch)], [("Sm", ch)])
+            if ch == 0:
+                clip(r, 1)
+            elif not last:
+                clip(r + 1, 0)
+            if last:
+                add("p", mm(NB[ch][0:64, 128:256], T.HS[:, ch * 64:ch * 64 + 64], T.P32[:, :]),
+                    r=[("H", ch), ("Sm", ch), "P32"], w=[("hsT", ch)], b=[("NB", ch)])
+            cp(offs(r + 1, ch), cnt, [("cnt", ch)], [("off", r + 1, ch)], [("NA", ch)])
+            for h in range(2):
+                (act if h else cp)(wide(T.Xg, ch, h), T.XI[:, 0:W].indirect(offs(r + 1, ch, h)),
+                                   ["X", ("off", r + 1, ch)], [("Xg", ch, h)])
+            bnew = T.bF[:, (r + 1) * 64 + ch * 32:(r + 1) * 64 + ch * 32 + 32]
+            act(bnew, cnt, [("cnt", ch)], [("bF", r + 1, ch)], [("NA", ch)])
+            oc = ch * 128
+            if last:
+                act(T.OH[0:32, oc:oc + 128], NB[ch][0:32, 128:256], [("hsT", ch)], [("OHh", ch)], [("NB", ch)])
+                act(T.OH[32:64, oc:oc + 128], NB[ch][32:64, 128:256], [("hsT", ch)], [("OHs", ch)], [("NB", ch)], scale=32.0)
+                if ch == 1:
+                    dma("y", T.yb[:, :], T.bF[:, RO * 64:RO * 64 + 64], [("bF", RO, 0), ("bF", RO, 1)], ["o_b"])
+                for blk in range(4):
+                    dma("y", T.yh[blk:128:4, 32 * ch:32 * ch + 32], T.OH[8 * blk:8 * blk + 8, oc:oc + 128],
+                        [("OHh", ch)], [("o_h", ch, blk)])
+                for blk in range(4):
+                    dma("y", T.ys[blk:128:4, 32 * ch:32 * ch + 32], T.OH[32 + 8 * blk:40 + 8 * blk, oc:oc + 128],
+                        [("OHs", ch)], [("o_s", ch, blk)])
+            xg = [("Xg", ch, 0), ("Xg", ch, 1)]
+            for s in range(2):
+                tt(wide(T.C2, ch, s), par(T.Xg, ch, s), PW[ch][s][:, 0:256], A.is_lt,
+                   xg + [("pw", ch, s)], [("C2", ch, s)], [("PW", ch, s)])
+                add("p", mm(PW[ch][s][:, 256:512], T.Sel[:, :], wide(T.C2, ch, s)),
+                    r=["Sel", ("C2", ch, s)], w=[("sel", ch, s)], b=[("PW", ch, s)])
+            for s in range(2):
+                c = ch * 512 + 256 * s
+                for h in range(2):
+                    tt(T.Yw[:, c + h:c + 256:2], quarter(T.Xg, ch, 2 * h + s), PW[ch][s][:, 256 + h:512:2],
+                       A.mult, xg + [("sel", ch, s)], [("Yw", ch, s, h)], [("PW", ch, s)])
+                    add("p", mm(redcol(ch, 2 * h + s), T.Yw[:, c + h:c + 256:2], T.Rm[:, :]),
+                        r=[("Yw", ch, s, h), "Rm"], w=[("red", ch, 2 * h + s)], b=[("NB", ch)])
+            red = [("red", ch, s) for s in range(4)]
+            if not last:
+                act(slot(r + 1, ch, rank), NB[ch][:, 0:32], red, [("own", r + 1, ch)], [("NB", ch)])
+                send(r + 1, ch)
+                gather_tops(r + 1, ch)
+            else:
+                cur = T.curT[:, ch * 32:ch * 32 + 32]
+                act(cur, NB[ch][:, 0:32], red, [("curT", ch)], [("NB", ch)])
+                add("p", mm(NB[ch][0:32, 256:384], cur, T.P32[:, :]), r=[("curT", ch), "P32"], w=[("cT", ch)], b=[("NB", ch)])
+                act(T.OC[0:32, oc:oc + 128], NB[ch][0:32, 256:384], [("cT", ch)], [("OC", ch)], [("NB", ch)], scale=32.0)
+                for blk in range(4):
+                    dma("s" if (ch == 1 and blk % 2 == 0) else "y", T.yc[blk:128:4, 32 * ch:32 * ch + 32],
+                        T.OC[8 * blk:8 * blk + 8, oc:oc + 128], [("OC", ch)], [("o_c", ch, blk)])
+    outs = ["o_b"] + [(n, ch, blk) for n in ("o_h", "o_s", "o_c") for ch in range(2) for blk in range(4)]
+    add("y", [], r=outs)
+    add("g", [], ext=[("sent", neng * RO * 2)])
+    emit(ops, Q, T)

@@ -9,22 +9,24 @@ BIG = float(2 ** 21)
 FILL_V = 1024
 FILL_S = 640
 TOP0 = 512
+SPLIT = True
+PLACE = [0, 1, 3, 4]
 NCS = 70
 NDS = 34
 
 SCRATCH = {n: ("sbuf", [128, c], d) for n, c, d in [
     ("sti", 64, "int32"), ("off", 64 * (RO + 1), "uint16"), ("bF", 64 * (RO + 1), "float32"),
     ("W0", W, "int32"), ("TI", W, "int32"), ("XI", W, "int32"),
-    ("Tg", 1024, "float32"), ("Xg", 1024, "float32"), ("Yw", 1024, "float32"),
+    ("Tg", 1024, "float32"), ("Xg", 1024, "float32"), ("Yw", 1024, "float32"), ("Pws", 1024, "float32"),
     ("C1", 1024, "bfloat16"), ("C2", 1024, "bfloat16"),
-    ("land", RO * 2 * NR * 32, "float32"), ("nar", 2 * 8 * 32, "float32"), ("HS", 128, "float32"), ("curT", 64, "float32"),
+    ("land", RO * 2 * 5 * 32, "float32"), ("nar", 2 * 8 * 32, "float32"), ("HS", 128, "float32"), ("curT", 64, "float32"),
     ("HL", 196, "float16"), ("PT", 256, "float16"), ("OH", 256, "float32"), ("OC", 256, "float32"),
     ("kI", 4, "int32"), ("kF", 16, "float32"), ("tF", 144, "float32"), ("td", 512, "float32"), ("tp", 128, "float32"),
     ("Bc", 144, "bfloat16"), ("sA", 128, "float32"), ("sB", 128, "float32"), ("Sel", 128, "bfloat16"),
     ("Wall", 512, "float16"), ("I16", 128, "float16"), ("I32", 128, "float32"), ("P32", 128, "float32"), ("Rm", 8, "float32")]}
 SCRATCH.update({n: ("psum", [128, 512], "float32") for n in ["PW00", "PW01", "PW10", "PW11", "NA0", "NA1", "NB0", "NB1"]})
 SEMAPHORES = (["c%d" % i for i in range(NCS)] + ["d%d" % i for i in range(NDS)] + ["sent"]
-              + ["a%d_%d_%d" % (r, ch, s) for r in range(RO) for ch in range(2) for s in range(NR)])
+              + ["a%d_%d" % (r, ch) for r in range(RO) for ch in range(2)])
 
 
 def emit(ops, Q, T):
@@ -133,7 +135,6 @@ def rank_program(g, core, T, topo):
         add("g", lambda: g.iota(out, pattern, 0, 0, allow_small_or_imprecise_dtypes=True), w=[key])
 
     peers = [(rank + k) % NR for k in range(1, NR)]
-    srcs = [(rank - k) % NR for k in range(1, NR)]
     mask = topo.mask(core, T.cores[peers[0]])
     for p in peers:
         mask &= topo.mask(core, T.cores[p])
@@ -143,14 +144,13 @@ def rank_program(g, core, T, topo):
         a = topo.addr(T.cores[p])
         dst_ids.append(DstId(rid=a[0], pnc=a[1]))
 
-    def slot(r, ch, s):
-        c = ((r * 2 + ch) * NR + s) * 32
-        return T.land[:, c:c + 32]
+    def slot(r, ch, place, n=1):
+        c = ((r * 2 + ch) * 5 + place) * 32
+        return T.land[:, c:c + 32 * n]
 
     def send(r, ch):
-        sl = slot(r, ch, rank)
-        tr = RemoteDMATransfer(dst_ids=dst_ids, dma_engine_mask=mask, remote_sem=T.sem["a%d_%d_%d" % (r, ch, rank)],
-                               srcs=[sl], dsts=[sl] * len(dst_ids))
+        tr = RemoteDMATransfer(dst_ids=dst_ids, dma_engine_mask=mask, remote_sem=T.sem["a%d_%d" % (r, ch)],
+                               srcs=[slot(r, ch, 0)], dsts=[slot(r, ch, PLACE[k]) for k in range(1, NR)])
         add("g", lambda: g.remote_dma_fused([tr], local_sem=T.sem.sent), r=[("own", r, ch)])
 
     PW = [[T.PW00, T.PW01], [T.PW10, T.PW11]]
@@ -170,21 +170,22 @@ def rank_program(g, core, T, topo):
     def par(buf, ch, s):
         return buf[:, ch * 512 + s:ch * 512 + 512:2]
 
-    def quarter(buf, ch, s):
-        return buf[:, ch * 512 + s:ch * 512 + 512:4]
+    def block(buf, ch, k):
+        c = ch * 512 + 256 * (k // 2)
+        return buf[:, c + k % 2:c + 256:2]
 
-    def redcol(ch, s):
-        return NB[ch][:, 8 * s:8 * s + 8]
+    def redcol(ch, k):
+        return NB[ch][:, 8 * k:8 * k + 8]
 
-    def narc(ch, i):
-        c = (ch * 8 + i) * 32
-        return T.nar[:, c:c + 32]
+    def ypart(y, ch, k):
+        c = 32 * ch + 16 * (k // 2)
+        return y[k % 2:128:2, c:c + 16]
 
     def gather_tops(r, ch):
         act(wide(T.Tg, ch), T.TI[:, 0:W].indirect(offs(r, ch)), ["T0", "T1", ("off", r, ch), "BG"], [("Tg", ch)], bias=BG)
 
     def clip(r, ch):
-        ts(narc(ch, 6), slot(r, ch, rank), (END - 1) / 32.0, None, A.min, None, [("own", r, ch)], [("nar", ch, 6)])
+        ts(slot(r, ch, 2), slot(r, ch, 0), (END - 1) / 32.0, None, A.min, None, [("own", r, ch)], [("clip", r, ch)])
 
     dma("y", T.sti[:, :], T.st[:, :], [], ["sti"])
     dma("y", T.TI[:, 0:TOP0], T.tops[:, 0:TOP0], [], ["T0"])
@@ -207,62 +208,62 @@ def rank_program(g, core, T, topo):
     ts(T.kI[:, 3:4], T.kI[:, 0:1], 31, None, A.bitwise_and, None, ["k0"], ["k3"])
     cp(kF[:, 0:4], T.kI[:, 0:4], ["k0", "k1", "k2", "k3"], ["kF"])
     ts(BG, KM, 15.0, BIG, A.is_equal, A.mult, ["kF"], ["BG"])
-    ts(K32B, K, 96.0, 1000.0, A.is_ge, A.mult, ["kF"], ["K32B"])
-    ts(WC, K, 64.0, 31.0, A.is_lt, A.mult, ["kF"], ["WC"])
     ts(T.Rm[:, :], T.tF[:, 0:128:16], KA, 1.0 / 32, A.is_equal, A.mult, ["tF", "kF"], ["Rm"])
     cp(T.off[:, 0:64], T.sti[:, :], ["sti"], [("off", 0, 0), ("off", 0, 1)])
     cp(T.bF[:, 0:64], T.sti[:, :], ["sti"], [("bF", 0, 0), ("bF", 0, 1)])
+    ts(K32B, K, 96.0, 1000.0, A.is_ge, A.mult, ["kF"], ["K32B"])
+    ts(WC, K, 64.0, 31.0, A.is_lt, A.mult, ["kF"], ["WC"])
     ts(TMP, BG, -16.0 / BIG, 1.0, A.mult, A.add, ["BG"], ["TMP"])
     tt(KK, BG, K, A.add, ["BG", "kF"], ["KK"])
-    tt(K32B, K32B, K32, A.add, ["K32B", "kF"], ["K32B"])
-    tt(NX, TMP, K, A.add, ["TMP", "kF"], ["NX"])
-    ts(WC, WC, 1.0, None, A.add, None, ["WC"], ["WC"])
     for ch in range(2):
         for h in range(2):
             win = T.W0[:, 0:W].indirect(offs(0, ch, h))
             (act if h else cp)(wide(T.Xg, ch, h), win, w0 + [("off", 0, ch)], [("Xg", ch, h)])
     for ch in range(2):
-        add("p", [mm(redcol(ch, s), quarter(T.Xg, ch, s), T.Rm[:, :]) for s in range(4)],
-            r=[("Xg", ch, 0), ("Xg", ch, 1), "Rm"], w=[("red", ch, s) for s in range(4)], b=[("NB", ch)])
-        cp(slot(0, ch, rank), NB[ch][:, 0:32], [("red", ch, s) for s in range(4)], [("own", 0, ch)], [("NB", ch)])
+        add("p", [mm(redcol(ch, k), block(T.Xg, ch, k), T.Rm[:, :]) for k in range(4)],
+            r=[("Xg", ch, 0), ("Xg", ch, 1), "Rm"], w=[("red", ch, 0), ("red", ch, 1)], b=[("NB", ch)])
+        cp(slot(0, ch, 0), NB[ch][:, 0:32], [("red", ch, 0), ("red", ch, 1)], [("own", 0, ch)], [("NB", ch)])
         send(0, ch)
         if ch == 0:
-            ts(T.HL[:, 96:196:98], kF[:, 0:2], 0.0, 32768.0, A.mult, A.add, ["kF"], ["HLc"])
-            ts(T.Bc[:, :], T.tF[:, :], 15.0, KA, A.subtract, A.is_equal, ["tF", "kF"], ["Bc"])
-            ts(T.I16[:, :], T.tF[:, 0:128], K, None, A.is_equal, None, ["tF", "kF"], ["I16"])
-    iota(T.tp[:, :], [[1, 4], [4, 32]], "tp")
+            tt(K32B, K32B, K32, A.add, ["K32B", "kF"], ["K32B"])
+            tt(NX, TMP, K, A.add, ["TMP", "kF"], ["NX"])
+            ts(WC, WC, 1.0, None, A.add, None, ["WC"], ["WC"])
+    iota(T.tp[:, :], [[1, 8], [8, 16]], "tp")
+    ts(T.HL[:, 96:196:98], kF[:, 0:2], 0.0, 32768.0, A.mult, A.add, ["kF"], ["HLc"])
+    ts(T.Bc[:, :], T.tF[:, :], 15.0, KA, A.subtract, A.is_equal, ["tF", "kF"], ["Bc"])
+    ts(T.I16[:, :], T.tF[:, 0:128], K, None, A.is_equal, None, ["tF", "kF"], ["I16"])
     ts(T.Wall[:, :], T.td[:, :], K32B, WC, A.is_equal, A.mult, ["td", "K32B", "WC"], ["Wall"])
     ts(T.I32[:, :], T.tF[:, 0:128], K, None, A.is_equal, None, ["tF", "kF"], ["I32"])
     ts(T.Wall[96:97, 15:512:16], T.td[96:97, 0:32], 0.0, 64.0, A.mult, A.add, ["td"], ["Wall"])
     ts(T.sA[:, :], T.tF[:, 0:128], NX, None, A.is_equal, None, ["tF", "NX"], ["sA"])
     ts(T.sB[:, :], T.tF[:, 0:128], KK, None, A.is_equal, None, ["tF", "KK"], ["sB"])
-    ts(T.P32[:, :], T.tp[:, :], K, None, A.is_equal, None, ["tp", "kF"], ["P32"])
+    clip(0, 0)
     tt(T.Sel[:, :], T.sA[:, :], T.sB[:, :], A.subtract, ["sA", "sB"], ["Sel"])
+    ts(T.P32[:, :], T.tp[:, :], K, None, A.is_equal, None, ["tp", "kF"], ["P32"])
     gather_tops(0, 0)
     gather_tops(0, 1)
-    clip(0, 0)
 
     for r in range(RO):
         last = r == RO - 1
         for ch in range(2):
-            def nar(i):
-                return narc(ch, i)
+            def nar(i, n=1):
+                c = (ch * 8 + i) * 32
+                return T.nar[:, c:c + 32 * n]
 
             def nk(i):
                 return ("nar", ch, i)
             hl = ch * 98
+            oc = ch * 128
             hi, lo, hit = [T.HL[:, hl + 32 * j:hl + 32 * j + 32] for j in range(3)]
-            mx, mn, mxk, mnk = slot(r, ch, rank), nar(6), ("own", r, ch), nk(6)
-            for j, s in enumerate(srcs):
-                arr = [("a%d_%d_%d" % (r, ch, s), neng)]
-                if j == NR - 2:
-                    tt(hi, mx, slot(r, ch, s), A.max, [mxk], [("hi", ch)], ext=arr)
-                    arr = []
-                tt(nar(j), mx, slot(r, ch, s), A.max, [mxk], [nk(j)], ext=arr)
-                tt(nar(3 + j), mn, slot(r, ch, s), A.min, [mnk], [nk(3 + j)])
-                mx, mn, mxk, mnk = nar(j), nar(3 + j), nk(j), nk(3 + j)
+            tt(nar(0, 2), slot(r, ch, 0, 2), slot(r, ch, 3, 2), A.max, [("own", r, ch)], [nk(0)],
+               ext=[("a%d_%d" % (r, ch), neng * (NR - 1))])
+            tt(nar(2, 2), slot(r, ch, 1, 2), slot(r, ch, 3, 2), A.min, [("clip", r, ch)], [nk(2)])
+            mx, mxk = nar(4), nk(4)
+            tt(hi, nar(0), nar(1), A.max, [nk(0)], [("hi", ch)])
+            tt(mx, nar(0), nar(1), A.max, [nk(0)], [mxk])
+            tt(nar(5), nar(2), nar(3), A.min, [nk(2)], [nk(5)])
             tt(lo, mx, hi, A.subtract, [mxk, ("hi", ch)], [("lo", ch)])
-            tt(hit, mx, mn, A.is_equal, [mxk, mnk], [("hit", ch)])
+            tt(hit, mx, nar(5), A.is_equal, [mxk, nk(5)], [("hit", ch)])
             add("p", mm(NA[ch][0:97, 0:128], T.HL[:, hl:hl + 97], T.I16[:, :]),
                 r=[("hi", ch), ("lo", ch), ("hit", ch), "HLc", "I16"], w=[("tr", ch)], b=[("NA", ch)])
             hcol = T.HS[:, ch * 64:ch * 64 + 32]
@@ -271,10 +272,10 @@ def rank_program(g, core, T, topo):
                 tt(scol, hit, mx, A.mult, [("hit", ch), mxk], [("Sm", ch)])
             else:
                 tt(nar(7), hit, mx, A.mult, [("hit", ch), mxk], [nk(7)])
-            pt = T.PT[0:97, ch * 128:ch * 128 + 128]
+            pt = T.PT[0:97, oc:oc + 128]
             cp(pt, NA[ch][0:97, 0:128], [("tr", ch)], [("PT", ch)], [("NA", ch)])
             for s in range(2):
-                add("p", [mm(PW[ch][s][:, h:256:2], T.Wall[0:97, 128 * (2 * h + s):128 * (2 * h + s) + 128], pt)
+                add("p", [mm(PW[ch][s][:, 128 * h:128 * h + 128], T.Wall[0:97, 128 * (2 * h + s):128 * (2 * h + s) + 128], pt)
                           for h in range(2)], r=[("PT", ch), "Wall"], w=[("pw", ch, s)], b=[("PW", ch, s)])
             cnt = NA[ch][:, 128:160]
             bold = T.bF[:, r * 64 + ch * 32:r * 64 + ch * 32 + 32]
@@ -285,54 +286,47 @@ def rank_program(g, core, T, topo):
                 tt(hcol, hcol, hit, A.add, [("hit", ch), ("H", ch)], [("H", ch)])
             for s in range(2):
                 c = ch * 512 + 256 * s
-                for h in range(2):
-                    tt(T.C1[:, c + h:c + 256:2], quarter(T.Tg, ch, 2 * h + s), PW[ch][s][:, h:256:2], A.is_lt,
-                       [("Tg", ch), ("pw", ch, s)], [("C1", ch, s, h)], [("PW", ch, s)])
+                for a, st in ([(0, 2), (1, 2)] if (SPLIT and s == 1) else [(0, 1)]):
+                    x0 = ch * 512 + 2 * a + s
+                    tt(T.C1[:, c + a:c + 256:st], T.Tg[:, x0:ch * 512 + 512:2 * st], PW[ch][s][:, a:256:st], A.is_lt,
+                       [("Tg", ch), ("pw", ch, s)], [("C1", ch, s, a)], [("PW", ch, s)])
                     add("p", [mm(cnt, T.Bc[:, 15 - 2 * j - s:143 - 2 * j - s], T.C1[:, c + j:c + 256:8], False, s == 1 and j == 7)
-                              for j in range(h, 8, 2)], r=["Bc", ("C1", ch, s, h)], w=[("cnt", ch)], b=[("NA", ch)], acc=True)
+                              for j in range(a, 8, st)], r=["Bc", ("C1", ch, s, a)], w=[("cnt", ch)], b=[("NA", ch)], acc=True)
+                act(par(T.Pws, ch, s), PW[ch][s][:, 0:256], [("pw", ch, s)], [("Pws", ch, s)], [("PW", ch, s)])
             if r > 0:
                 tt(scol, scol, nar(7), A.add, [nk(7), ("Sm", ch)], [("Sm", ch)])
-            if ch == 0:
-                clip(r, 1)
-            elif not last:
-                clip(r + 1, 0)
+            if ch == 0 or not last:
+                clip(r + ch, 1 - ch)
             if last:
                 add("p", mm(NB[ch][0:64, 128:256], T.HS[:, ch * 64:ch * 64 + 64], T.P32[:, :]),
                     r=[("H", ch), ("Sm", ch), "P32"], w=[("hsT", ch)], b=[("NB", ch)])
             cp(offs(r + 1, ch), cnt, [("cnt", ch)], [("off", r + 1, ch)], [("NA", ch)])
             for h in range(2):
-                (act if h else cp)(wide(T.Xg, ch, h), T.XI[:, 0:W].indirect(offs(r + 1, ch, h)),
-                                   ["X", ("off", r + 1, ch)], [("Xg", ch, h)])
+                win = T.XI[:, 0:W].indirect(offs(r + 1, ch, h))
+                tt(wide(T.C2, ch, h), win, wide(T.Pws, ch, h), A.is_lt,
+                   ["X", ("off", r + 1, ch), ("Pws", ch, 0), ("Pws", ch, 1)], [("C2", ch, h)])
+                act(wide(T.Xg, ch, h), win, ["X", ("off", r + 1, ch)], [("Xg", ch, h)])
+                add("p", mm(PW[ch][h][:, 256:512], T.Sel[:, :], wide(T.C2, ch, h)),
+                    r=["Sel", ("C2", ch, h)], w=[("sel", ch, h)], b=[("PW", ch, h)])
             bnew = T.bF[:, (r + 1) * 64 + ch * 32:(r + 1) * 64 + ch * 32 + 32]
-            act(bnew, cnt, [("cnt", ch)], [("bF", r + 1, ch)], [("NA", ch)])
-            oc = ch * 128
             if last:
                 act(T.OH[0:32, oc:oc + 128], NB[ch][0:32, 128:256], [("hsT", ch)], [("OHh", ch)], [("NB", ch)])
                 act(T.OH[32:64, oc:oc + 128], NB[ch][32:64, 128:256], [("hsT", ch)], [("OHs", ch)], [("NB", ch)], scale=32.0)
-                if ch == 1:
-                    dma("y", T.yb[:, :], T.bF[:, RO * 64:RO * 64 + 64], [("bF", RO, 0), ("bF", RO, 1)], ["o_b"])
-                for blk in range(4):
-                    dma("y", T.yh[blk:128:4, 32 * ch:32 * ch + 32], T.OH[8 * blk:8 * blk + 8, oc:oc + 128],
-                        [("OHh", ch)], [("o_h", ch, blk)])
-                for blk in range(4):
-                    dma("y", T.ys[blk:128:4, 32 * ch:32 * ch + 32], T.OH[32 + 8 * blk:40 + 8 * blk, oc:oc + 128],
-                        [("OHs", ch)], [("o_s", ch, blk)])
-            xg = [("Xg", ch, 0), ("Xg", ch, 1)]
-            for s in range(2):
-                tt(wide(T.C2, ch, s), par(T.Xg, ch, s), PW[ch][s][:, 0:256], A.is_lt,
-                   xg + [("pw", ch, s)], [("C2", ch, s)], [("PW", ch, s)])
-                add("p", mm(PW[ch][s][:, 256:512], T.Sel[:, :], wide(T.C2, ch, s)),
-                    r=["Sel", ("C2", ch, s)], w=[("sel", ch, s)], b=[("PW", ch, s)])
-            for s in range(2):
-                c = ch * 512 + 256 * s
-                for h in range(2):
-                    tt(T.Yw[:, c + h:c + 256:2], quarter(T.Xg, ch, 2 * h + s), PW[ch][s][:, 256 + h:512:2],
-                       A.mult, xg + [("sel", ch, s)], [("Yw", ch, s, h)], [("PW", ch, s)])
-                    add("p", mm(redcol(ch, 2 * h + s), T.Yw[:, c + h:c + 256:2], T.Rm[:, :]),
-                        r=[("Yw", ch, s, h), "Rm"], w=[("red", ch, 2 * h + s)], b=[("NB", ch)])
-            red = [("red", ch, s) for s in range(4)]
+                for k in range(4):
+                    dma("y", ypart(T.yh, ch, k), T.OH[8 * k:8 * k + 8, oc:oc + 128], [("OHh", ch)], [("o_h", ch, k)])
+                for k in range(4):
+                    dma("y", ypart(T.ys, ch, k), T.OH[32 + 8 * k:40 + 8 * k, oc:oc + 128], [("OHs", ch)], [("o_s", ch, k)])
+            act(bnew, cnt, [("cnt", ch)], [("bF", r + 1, ch)], [("NA", ch)])
+            if last and ch == 1:
+                dma("s", T.yb[:, :], T.bF[:, RO * 64:RO * 64 + 64], [("bF", RO, 0), ("bF", RO, 1)], ["o_b"])
+            for h in range(2):
+                tt(wide(T.Yw, ch, h), wide(T.Xg, ch, h), PW[ch][h][:, 256:512], A.mult,
+                   [("Xg", ch, h), ("sel", ch, h)], [("Yw", ch, h)], [("PW", ch, h)])
+                add("p", [mm(redcol(ch, 2 * h + s), block(T.Yw, ch, 2 * h + s), T.Rm[:, :]) for s in range(2)],
+                    r=[("Yw", ch, h), "Rm"], w=[("red", ch, h)], b=[("NB", ch)])
+            red = [("red", ch, 0), ("red", ch, 1)]
             if not last:
-                act(slot(r + 1, ch, rank), NB[ch][:, 0:32], red, [("own", r + 1, ch)], [("NB", ch)])
+                act(slot(r + 1, ch, 0), NB[ch][:, 0:32], red, [("own", r + 1, ch)], [("NB", ch)])
                 send(r + 1, ch)
                 gather_tops(r + 1, ch)
             else:
@@ -340,10 +334,10 @@ def rank_program(g, core, T, topo):
                 act(cur, NB[ch][:, 0:32], red, [("curT", ch)], [("NB", ch)])
                 add("p", mm(NB[ch][0:32, 256:384], cur, T.P32[:, :]), r=[("curT", ch), "P32"], w=[("cT", ch)], b=[("NB", ch)])
                 act(T.OC[0:32, oc:oc + 128], NB[ch][0:32, 256:384], [("cT", ch)], [("OC", ch)], [("NB", ch)], scale=32.0)
-                for blk in range(4):
-                    dma("s" if (ch == 1 and blk % 2 == 0) else "y", T.yc[blk:128:4, 32 * ch:32 * ch + 32],
-                        T.OC[8 * blk:8 * blk + 8, oc:oc + 128], [("OC", ch)], [("o_c", ch, blk)])
-    outs = ["o_b"] + [(n, ch, blk) for n in ("o_h", "o_s", "o_c") for ch in range(2) for blk in range(4)]
+                for k in range(4):
+                    dma("s" if (ch == 1 and k % 2 == 0) else "y", ypart(T.yc, ch, k),
+                        T.OC[8 * k:8 * k + 8, oc:oc + 128], [("OC", ch)], [("o_c", ch, k)])
+    outs = ["o_b"] + [(n, ch, k) for n in ("o_h", "o_s", "o_c") for ch in range(2) for k in range(4)]
     add("y", [], r=outs)
     add("g", [], ext=[("sent", neng * RO * 2)])
     emit(ops, Q, T)

from concourse.bass import DstId, RemoteDMATransfer
from concourse.mybir import AluOpType, ActivationFunctionType

NR = 4
RO = 4
W = 2048
END = 2 ** 20 - 1
BIG = float(2 ** 21)
FILL_V = 1024
FILL_S = 640
TOP0 = 512
SPLIT = True
PLACE = [0, 1, 3, 4]
NCS = 70
NDS = 34

SCRATCH = {n: ("sbuf", [128, c], d) for n, c, d in [
    ("sti", 64, "int32"), ("off", 64 * (RO + 1), "uint16"), ("bF", 64 * (RO + 1), "float32"),
    ("W0", W, "int32"), ("TI", W, "int32"), ("XI", W, "int32"),
    ("Tg", 1024, "float32"), ("Xg", 1024, "float32"), ("Yw", 1024, "float32"), ("Pws", 1024, "float32"),
    ("C1", 1024, "bfloat16"), ("C2", 1024, "bfloat16"),
    ("land", RO * 2 * 5 * 32, "float32"), ("nar", 2 * 8 * 32, "float32"), ("HS", 128, "float32"), ("curT", 64, "float32"),
    ("HL", 196, "float16"), ("PT", 256, "float16"), ("OH", 256, "float32"), ("OC", 256, "float32"),
    ("kI", 4, "int32"), ("kF", 16, "float32"), ("tF", 144, "float32"), ("td", 512, "float32"), ("tp", 128, "float32"),
    ("Bc", 144, "bfloat16"), ("sA", 128, "float32"), ("sB", 128, "float32"), ("Sel", 128, "bfloat16"),
    ("Wall", 512, "float16"), ("I16", 128, "float16"), ("I32", 128, "float32"), ("P32", 128, "float32"), ("Rm", 8, "float32")]}
SCRATCH.update({n: ("psum", [128, 512], "float32") for n in ["PW00", "PW01", "PW10", "PW11", "NA0", "NA1", "NB0", "NB1"]})
SEMAPHORES = (["c%d" % i for i in range(NCS)] + ["d%d" % i for i in range(NDS)] + ["sent"]
              + ["a%d_%d" % (r, ch) for r in range(RO) for ch in range(2)])


def emit(ops, Q, T):
    writers, readers, bank = {}, {}, {}
    known = {q: 0 for q in Q}
    for n, op in enumerate(ops):
        q = op["q"]
        deps = set()
        for k in op["r"]:
            deps.update(writers.get(k, []))
        for k in op["w"]:
            deps.update(readers.get(k, []))
            deps.update(writers.get(k, []))
        for b in op["b"]:
            run = bank.get(b)
            if run is None or run[0] != q:
                if run is not None:
                    deps.update(run[1])
                bank[b] = (q, [n], run[1] if run is not None else [])
            else:
                deps.update(run[2])
                run[1].append(n)
        if q == "p":
            deps = set(d for d in deps if ops[d]["q"] != "p")
        deps.discard(n)
        waits = []
        for d in sorted(deps, reverse=True):
            if not (known[q] >> d) & 1:
                waits.append(d)
                ops[d]["waited"] = True
                known[q] |= ops[d]["hb"] | (1 << d)
        op["waits"] = waits
        op["hb"] = known[q]
        for k in op["r"]:
            readers.setdefault(k, []).append(n)
        for k in op["w"]:
            if op["acc"]:
                writers.setdefault(k, []).append(n)
            else:
                writers[k] = [n]
            readers[k] = []
    pools = {False: [["c%d" % i, -1, 0] for i in range(NCS)], True: [["d%d" % i, -1, 0] for i in range(NDS)]}
    for n, op in enumerate(ops):
        eng = Q[op["q"]]
        for d in reversed(op["waits"]):
            eng.wait_ge(T.sem[ops[d]["sem"]], ops[d]["val"])
        for name, val in op["ext"]:
            eng.wait_ge(T.sem[name], val)
        slot = None
        if op["waited"]:
            for s in pools[op["dma"]]:
                if s[1] < 0 or (op["hb"] >> s[1]) & 1:
                    slot = s
                    break
            assert slot is not None
        for f in op["fn"]:
            ins = f()
            if slot is not None:
                inc = 16 if op["dma"] else 1
                ins.then_inc(T.sem[slot[0]], inc)
                slot[2] += inc
        if slot is not None:
            slot[1] = n
            op["sem"], op["val"] = slot[0], slot[2]


def rank_program(g, core, T, topo):
    rank = T.rank_of(core)
    if rank is None:
        return
    A = AluOpType
    ACT = ActivationFunctionType
    V, S, P, Y = g.vector, g.scalar, g.tensor, g.sync
    Q = {"v": V, "s": S, "p": P, "g": g, "y": Y}
    ops = []

    def add(q, fn, r=(), w=(), b=(), ext=(), dma=False, acc=False):
        ops.append({"q": q, "fn": fn if isinstance(fn, list) else [fn], "r": list(r), "w": list(w), "b": list(b),
                    "ext": list(ext), "dma": dma, "acc": acc, "waited": False})

    def ts(out, in0, s1, s2, o0, o1, r, w, b=()):
        if o1 is None:
            add("v", lambda: V.tensor_scalar(out, in0, s1, None, o0), r, w, b)
        else:
            add("v", lambda: V.tensor_scalar(out, in0, s1, s2, o0, o1), r, w, b)

    def tt(out, in0, in1, o, r, w, b=(), ext=()):
        add("v", lambda: V.tensor_tensor(out, in0, in1, o), r, w, b, ext)

    def cp(out, in_, r, w, b=()):
        add("v", lambda: V.tensor_copy(out, in_), r, w, b)

    def act(out, in_, r, w, b=(), scale=1.0, bias=None):
        if bias is None:
            add("s", lambda: S.activation(out, in_, ACT.Identity, scale=scale), r, w, b)
        else:
            add("s", lambda: S.activation(out, in_, ACT.Identity, bias=bias), r, w, b)

    def mm(out, lhsT, rhs, start=True, stop=True):
        return lambda: P.matmul(out, lhsT, rhs, start, stop)

    def dma(q, out, in_, r, w, ext=()):
        add(q, lambda: Q[q].dma_start(out, in_), r, w, (), ext, dma=True)

    def iota(out, pattern, key):
        add("g", lambda: g.iota(out, pattern, 0, 0, allow_small_or_imprecise_dtypes=True), w=[key])

    peers = [(rank + k) % NR for k in range(1, NR)]
    mask = topo.mask(core, T.cores[peers[0]])
    for p in peers:
        mask &= topo.mask(core, T.cores[p])
    neng = bin(mask).count("1")
    dst_ids = []
    for p in peers:
        a = topo.addr(T.cores[p])
        dst_ids.append(DstId(rid=a[0], pnc=a[1]))

    def slot(r, ch, place, n=1):
        c = ((r * 2 + ch) * 5 + place) * 32
        return T.land[:, c:c + 32 * n]

    def send(r, ch):
        tr = RemoteDMATransfer(dst_ids=dst_ids, dma_engine_mask=mask, remote_sem=T.sem["a%d_%d" % (r, ch)],
                               srcs=[slot(r, ch, 0)], dsts=[slot(r, ch, PLACE[k]) for k in range(1, NR)])
        add("g", lambda: g.remote_dma_fused([tr], local_sem=T.sem.sent), r=[("own", r, ch)])

    PW = [[T.PW00, T.PW01], [T.PW10, T.PW11]]
    NA = [T.NA0, T.NA1]
    NB = [T.NB0, T.NB1]
    kF = T.kF
    K, KA, KM, K32, BG, NX, KK, K32B, TMP, WC = [kF[:, i:i + 1] for i in range(10)]

    def offs(r, ch, h=None):
        c = r * 64 + ch * 32
        return T.off[:, c:c + 32] if h is None else T.off[:, c + 16 * h:c + 16 * h + 16]

    def wide(buf, ch, h=None):
        c = ch * 512
        return buf[:, c:c + 512] if h is None else buf[:, c + 256 * h:c + 256 * h + 256]

    def par(buf, ch, s):
        return buf[:, ch * 512 + s:ch * 512 + 512:2]

    def block(buf, ch, k):
        c = ch * 512 + 256 * (k // 2)
        return buf[:, c + k % 2:c + 256:2]

    def redcol(ch, k):
        return NB[ch][:, 8 * k:8 * k + 8]

    def ypart(y, ch, k):
        c = 32 * ch + 16 * (k // 2)
        return y[k % 2:128:2, c:c + 16]

    def gather_tops(r, ch):
        act(wide(T.Tg, ch), T.TI[:, 0:W].indirect(offs(r, ch)), ["T0", "T1", ("off", r, ch), "BG"], [("Tg", ch)], bias=BG)

    def clip(r, ch):
        ts(slot(r, ch, 2), slot(r, ch, 0), (END - 1) / 32.0, None, A.min, None, [("own", r, ch)], [("clip", r, ch)])

    dma("y", T.sti[:, :], T.st[:, :], [], ["sti"])
    dma("y", T.TI[:, 0:TOP0], T.tops[:, 0:TOP0], [], ["T0"])
    add("v", lambda: V.memset(T.W0[:, 0:256], 0), w=["W0a"])
    add("v", lambda: V.memset(T.W0[:, 256:FILL_V], 0), w=["W0b"])
    add("g", lambda: g.iota(T.W0[:, FILL_V + FILL_S:W], [[0, W - FILL_V - FILL_S]], 0, 0), w=["W0c"])
    w0 = ["W0a", "W0b", "W0c"]
    for c in range(FILL_V, FILL_V + FILL_S, 256):
        n = min(256, FILL_V + FILL_S - c)
        act(T.W0[:, c:c + n], T.W0[:, 0:n], ["W0a"], [("W0", c)])
        w0.append(("W0", c))
    dma("y", T.W0[0:128:16, :], T.ids[0:128:16, :], [], w0)
    dma("y", T.TI[:, TOP0:W], T.tops[:, TOP0:W], [], ["T1"])
    dma("y", T.XI[:, :], T.ids[:, :], [], ["X"])
    add("g", lambda: g.iota(T.kI[:, 0:1], [[0, 1]], 0, 1), w=["k0"])
    iota(T.tF[:, :], [[1, 144]], "tF")
    iota(T.td[:, :], [[1, 32], [0, 16]], "td")
    ts(T.kI[:, 1:2], T.kI[:, 0:1], 112, None, A.bitwise_and, None, ["k0"], ["k1"])
    ts(T.kI[:, 2:3], T.kI[:, 0:1], 15, None, A.bitwise_and, None, ["k0"], ["k2"])
    ts(T.kI[:, 3:4], T.kI[:, 0:1], 31, None, A.bitwise_and, None, ["k0"], ["k3"])
    cp(kF[:, 0:4], T.kI[:, 0:4], ["k0", "k1", "k2", "k3"], ["kF"])
    ts(BG, KM, 15.0, BIG, A.is_equal, A.mult, ["kF"], ["BG"])
    ts(T.Rm[:, :], T.tF[:, 0:128:16], KA, 1.0 / 32, A.is_equal, A.mult, ["tF", "kF"], ["Rm"])
    cp(T.off[:, 0:64], T.sti[:, :], ["sti"], [("off", 0, 0), ("off", 0, 1)])
    cp(T.bF[:, 0:64], T.sti[:, :], ["sti"], [("bF", 0, 0), ("bF", 0, 1)])
    ts(K32B, K, 96.0, 1000.0, A.is_ge, A.mult, ["kF"], ["K32B"])
    ts(WC, K, 64.0, 31.0, A.is_lt, A.mult, ["kF"], ["WC"])
    ts(TMP, BG, -16.0 / BIG, 1.0, A.mult, A.add, ["BG"], ["TMP"])
    tt(KK, BG, K, A.add, ["BG", "kF"], ["KK"])
    for ch in range(2):
        for h in range(2):
            win = T.W0[:, 0:W].indirect(offs(0, ch, h))
            (act if h else cp)(wide(T.Xg, ch, h), win, w0 + [("off", 0, ch)], [("Xg", ch, h)])
    for ch in range(2):
        add("p", [mm(redcol(ch, k), block(T.Xg, ch, k), T.Rm[:, :]) for k in range(4)],
            r=[("Xg", ch, 0), ("Xg", ch, 1), "Rm"], w=[("red", ch, 0), ("red", ch, 1)], b=[("NB", ch)])
        cp(slot(0, ch, 0), NB[ch][:, 0:32], [("red", ch, 0), ("red", ch, 1)], [("own", 0, ch)], [("NB", ch)])
        send(0, ch)
        if ch == 0:
            tt(K32B, K32B, K32, A.add, ["K32B", "kF"], ["K32B"])
            tt(NX, TMP, K, A.add, ["TMP", "kF"], ["NX"])
            ts(WC, WC, 1.0, None, A.add, None, ["WC"], ["WC"])
    iota(T.tp[:, :], [[1, 8], [8, 16]], "tp")
    ts(T.HL[:, 96:196:98], kF[:, 0:2], 0.0, 32768.0, A.mult, A.add, ["kF"], ["HLc"])
    ts(T.Bc[:, :], T.tF[:, :], 15.0, KA, A.subtract, A.is_equal, ["tF", "kF"], ["Bc"])
    ts(T.I16[:, :], T.tF[:, 0:128], K, None, A.is_equal, None, ["tF", "kF"], ["I16"])
    ts(T.Wall[:, :], T.td[:, :], K32B, WC, A.is_equal, A.mult, ["td", "K32B", "WC"], ["Wall"])
    ts(T.I32[:, :], T.tF[:, 0:128], K, None, A.is_equal, None, ["tF", "kF"], ["I32"])
    ts(T.Wall[96:97, 15:512:16], T.td[96:97, 0:32], 0.0, 64.0, A.mult, A.add, ["td"], ["Wall"])
    ts(T.sA[:, :], T.tF[:, 0:128], NX, None, A.is_equal, None, ["tF", "NX"], ["sA"])
    ts(T.sB[:, :], T.tF[:, 0:128], KK, None, A.is_equal, None, ["tF", "KK"], ["sB"])
    clip(0, 0)
    tt(T.Sel[:, :], T.sA[:, :], T.sB[:, :], A.subtract, ["sA", "sB"], ["Sel"])
    ts(T.P32[:, :], T.tp[:, :], K, None, A.is_equal, None, ["tp", "kF"], ["P32"])
    gather_tops(0, 0)
    gather_tops(0, 1)

    for r in range(RO):
        last = r == RO - 1
        for ch in range(2):
            def nar(i, n=1):
                c = (ch * 8 + i) * 32
                return T.nar[:, c:c + 32 * n]

            def nk(i):
                return ("nar", ch, i)
            hl = ch * 98
            oc = ch * 128
            hi, lo, hit = [T.HL[:, hl + 32 * j:hl + 32 * j + 32] for j in range(3)]
            tt(nar(0, 2), slot(r, ch, 0, 2), slot(r, ch, 3, 2), A.max, [("own", r, ch)], [nk(0)],
               ext=[("a%d_%d" % (r, ch), neng * (NR - 1))])
            tt(nar(2, 2), slot(r, ch, 1, 2), slot(r, ch, 3, 2), A.min, [("clip", r, ch)], [nk(2)])
            mx, mxk = nar(4), nk(4)
            tt(hi, nar(0), nar(1), A.max, [nk(0)], [("hi", ch)])
            tt(mx, nar(0), nar(1), A.max, [nk(0)], [mxk])
            tt(nar(5), nar(2), nar(3), A.min, [nk(2)], [nk(5)])
            tt(lo, mx, hi, A.subtract, [mxk, ("hi", ch)], [("lo", ch)])
            tt(hit, mx, nar(5), A.is_equal, [mxk, nk(5)], [("hit", ch)])
            add("p", mm(NA[ch][0:97, 0:128], T.HL[:, hl:hl + 97], T.I16[:, :]),
                r=[("hi", ch), ("lo", ch), ("hit", ch), "HLc", "I16"], w=[("tr", ch)], b=[("NA", ch)])
            hcol = T.HS[:, ch * 64:ch * 64 + 32]
            scol = T.HS[:, ch * 64 + 32:ch * 64 + 64]
            if r == 0:
                tt(scol, hit, mx, A.mult, [("hit", ch), mxk], [("Sm", ch)])
            else:
                tt(nar(7), hit, mx, A.mult, [("hit", ch), mxk], [nk(7)])
            pt = T.PT[0:97, oc:oc + 128]
            cp(pt, NA[ch][0:97, 0:128], [("tr", ch)], [("PT", ch)], [("NA", ch)])
            for s in range(2):
                add("p", [mm(PW[ch][s][:, 128 * h:128 * h + 128], T.Wall[0:97, 128 * (2 * h + s):128 * (2 * h + s) + 128], pt)
                          for h in range(2)], r=[("PT", ch), "Wall"], w=[("pw", ch, s)], b=[("PW", ch, s)])
            cnt = NA[ch][:, 128:160]
            bold = T.bF[:, r * 64 + ch * 32:r * 64 + ch * 32 + 32]
            add("p", mm(cnt, T.I32[:, :], bold, True, False), r=["I32", ("bF", r, ch)], w=[("cnt", ch)], b=[("NA", ch)])
            if r == 0:
                cp(hcol, hit, [("hit", ch)], [("H", ch)])
            else:
                tt(hcol, hcol, hit, A.add, [("hit", ch), ("H", ch)], [("H", ch)])
            for s in range(2):
                c = ch * 512 + 256 * s
                for a, st in ([(0, 2), (1, 2)] if (SPLIT and s == 1) else [(0, 1)]):
                    x0 = ch * 512 + 2 * a + s
                    tt(T.C1[:, c + a:c + 256:st], T.Tg[:, x0:ch * 512 + 512:2 * st], PW[ch][s][:, a:256:st], A.is_lt,
                       [("Tg", ch), ("pw", ch, s)], [("C1", ch, s, a)], [("PW", ch, s)])
                    add("p", [mm(cnt, T.Bc[:, 15 - 2 * j - s:143 - 2 * j - s], T.C1[:, c + j:c + 256:8], False, s == 1 and j == 7)
                              for j in range(a, 8, st)], r=["Bc", ("C1", ch, s, a)], w=[("cnt", ch)], b=[("NA", ch)], acc=True)
                act(par(T.Pws, ch, s), PW[ch][s][:, 0:256], [("pw", ch, s)], [("Pws", ch, s)], [("PW", ch, s)])
            if r > 0:
                tt(scol, scol, nar(7), A.add, [nk(7), ("Sm", ch)], [("Sm", ch)])
            if ch == 0 or not last:
                clip(r + ch, 1 - ch)
            if last:
                add("p", mm(NB[ch][0:64, 128:256], T.HS[:, ch * 64:ch * 64 + 64], T.P32[:, :]),
                    r=[("H", ch), ("Sm", ch), "P32"], w=[("hsT", ch)], b=[("NB", ch)])
            cp(offs(r + 1, ch), cnt, [("cnt", ch)], [("off", r + 1, ch)], [("NA", ch)])
            for h in range(2):
                win = T.XI[:, 0:W].indirect(offs(r + 1, ch, h))
                tt(wide(T.C2, ch, h), win, wide(T.Pws, ch, h), A.is_lt,
                   ["X", ("off", r + 1, ch), ("Pws", ch, 0), ("Pws", ch, 1)], [("C2", ch, h)])
                act(wide(T.Xg, ch, h), win, ["X", ("off", r + 1, ch)], [("Xg", ch, h)])
                add("p", mm(PW[ch][h][:, 256:512], T.Sel[:, :], wide(T.C2, ch, h)),
                    r=["Sel", ("C2", ch, h)], w=[("sel", ch, h)], b=[("PW", ch, h)])
            bnew = T.bF[:, (r + 1) * 64 + ch * 32:(r + 1) * 64 + ch * 32 + 32]
            if last:
                act(T.OH[0:32, oc:oc + 128], NB[ch][0:32, 128:256], [("hsT", ch)], [("OHh", ch)], [("NB", ch)])
                act(T.OH[32:64, oc:oc + 128], NB[ch][32:64, 128:256], [("hsT", ch)], [("OHs", ch)], [("NB", ch)], scale=32.0)
                for k in range(4):
                    dma("y", ypart(T.yh, ch, k), T.OH[8 * k:8 * k + 8, oc:oc + 128], [("OHh", ch)], [("o_h", ch, k)])
                for k in range(4):
                    dma("y", ypart(T.ys, ch, k), T.OH[32 + 8 * k:40 + 8 * k, oc:oc + 128], [("OHs", ch)], [("o_s", ch, k)])
            act(bnew, cnt, [("cnt", ch)], [("bF", r + 1, ch)], [("NA", ch)])
            if last and ch == 1:
                dma("s", T.yb[:, :], T.bF[:, RO * 64:RO * 64 + 64], [("bF", RO, 0), ("bF", RO, 1)], ["o_b"])
            for h in range(2):
                tt(wide(T.Yw, ch, h), wide(T.Xg, ch, h), PW[ch][h][:, 256:512], A.mult,
                   [("Xg", ch, h), ("sel", ch, h)], [("Yw", ch, h)], [("PW", ch, h)])
                add("p", [mm(redcol(ch, 2 * h + s), block(T.Yw, ch, 2 * h + s), T.Rm[:, :]) for s in range(2)],
                    r=[("Yw", ch, h), "Rm"], w=[("red", ch, h)], b=[("NB", ch)])
            red = [("red", ch, 0), ("red", ch, 1)]
            if not last:
                act(slot(r + 1, ch, 0), NB[ch][:, 0:32], red, [("own", r + 1, ch)], [("NB", ch)])
                send(r + 1, ch)
                gather_tops(r + 1, ch)
            else:
                cur = T.curT[:, ch * 32:ch * 32 + 32]
                act(cur, NB[ch][:, 0:32], red, [("curT", ch)], [("NB", ch)])
                add("p", mm(NB[ch][0:32, 256:384], cur, T.P32[:, :]), r=[("curT", ch), "P32"], w=[("cT", ch)], b=[("NB", ch)])
                act(T.OC[0:32, oc:oc + 128], NB[ch][0:32, 256:384], [("cT", ch)], [("OC", ch)], [("NB", ch)], scale=32.0)
                for k in range(4):
                    dma("s" if (ch == 1 and k % 2 == 0) else "y", ypart(T.yc, ch, k),
                        T.OC[8 * k:8 * k + 8, oc:oc + 128], [("OC", ch)], [("o_c", ch, k)])
    outs = ["o_b"] + [(n, ch, k) for n in ("o_h", "o_s", "o_c") for ch in range(2) for k in range(4)]
    add("y", [], r=outs)
    add("g", [], ext=[("sent", neng * RO * 2)])
    emit(ops, Q, T)
